import numpy as np
import ml_dtypes


def mxq(x, axis, fmt="e4m3"):
    dtype, down = {"e4m3": (ml_dtypes.float8_e4m3fn, 7), "e5m2": (ml_dtypes.float8_e5m2, 14)}[fmt]
    v = np.moveaxis(np.asarray(x, np.float32).astype(ml_dtypes.bfloat16).astype(np.float64), axis, -1)
    blocks = v.reshape(v.shape[:-1] + (-1, 32))
    amax = np.abs(blocks).max(-1, keepdims=True)
    byte = np.maximum(np.where(amax > 0, np.frexp(amax)[1] - 1 + 127, 0) - down, 1)
    scale = np.exp2(byte - 127.0)
    codes = (blocks / scale).astype(np.float32).astype(dtype).astype(np.float64)
    return np.moveaxis((codes * scale).reshape(v.shape), -1, axis)


WIDE = False


def mx_kscale(k):
    if not WIDE:
        return np.ones(k)
    levels = np.array([10, -10, 5, -5, 0])
    if k % 512:
        return np.exp2(np.random.permutation(np.resize(levels, k // 32))).repeat(32)
    a = np.empty((k // 512, 16))
    for p in range(k // 512):
        a[p, :8] = np.random.permutation(np.resize(levels, 8))
        for g in range(8):
            far = levels[np.abs(levels - a[p, g]) >= 10]
            a[p, g + 8] = far[np.random.randint(len(far))]
    return np.exp2(a.ravel()).repeat(32)


def f64(x):
    return np.asarray(x).astype(np.float64)


def striped(idx):
    return np.tile(idx.reshape(-1, 16).T, (8, 1)).astype(np.uint16)


def unstriped(offs):
    return offs[:16].T.reshape(-1).astype(np.int64)


def striped8(idx):
    return np.concatenate([x.reshape(-1, 16).T for x in idx]).astype(np.uint16)


def runs(offs, k):
    lists = np.stack([offs[16 * r : 16 * r + 16].T.reshape(-1) for r in range(8)]).astype(np.int64)
    return lists[np.arange(k) % 512 // 64]


def pack_weight(w):
    k, n = w.shape
    w = f64(np.asarray(w, np.float32).astype(ml_dtypes.bfloat16)).reshape(k // 32, 32, n)
    amax = np.abs(w).max(1)
    byte = np.clip(np.where(amax > 0, np.frexp(amax)[1] - 1 + 127 - 7, 1), 1, 254)
    scaled = (w * np.exp2(127.0 - byte)[:, None, :]).reshape(k, n).astype(np.float32)
    words = np.ascontiguousarray(scaled.reshape(k // 512, 128, 4, n).transpose(0, 1, 3, 2)).astype(ml_dtypes.float8_e4m3fn).view(np.uint8)
    return words, np.ascontiguousarray(byte.astype(np.uint8).reshape(k // 512, 16, n))


def unpack_weight(words, scales):
    g, p, n, _ = words.shape
    vals = np.ascontiguousarray(words).view(ml_dtypes.float8_e4m3fn).astype(np.float64) * np.repeat(np.exp2(scales.astype(np.float64) - 127.0), 8, axis=1)[..., None]
    return vals.transpose(0, 1, 3, 2).reshape(g * 512, n)


E2M1 = np.array([0.0, 0.5, 1.0, 1.5, 2.0, 3.0, 4.0, 6.0, -0.0, -0.5, -1.0, -1.5, -2.0, -3.0, -4.0, -6.0])


def pack_fp4(w):
    k, n = w.shape
    w = f64(np.asarray(w, np.float32).astype(ml_dtypes.bfloat16)).reshape(k // 32, 32, n)
    amax = np.abs(w).max(1)
    mant, ex = np.frexp(amax / 6.0)
    byte = np.clip(np.where(amax > 0, np.where(mant > 0.5, ex, ex - 1) + 127, 1), 1, 254)
    scaled = (w * np.exp2(127.0 - byte)[:, None, :]).reshape(k, n).astype(np.float32)
    c = np.ascontiguousarray(scaled.reshape(k // 512, 128, 4, n).transpose(0, 1, 3, 2)).astype(ml_dtypes.float4_e2m1fn).view(np.uint8) & 0xF
    words = (c[..., 0::2] | (c[..., 1::2] << 4)).reshape(k // 512, 128, 2 * n)
    return np.ascontiguousarray(words), np.ascontiguousarray(byte.astype(np.uint8).reshape(k // 512, 16, n))


def unpack_fp4(words, scales):
    g, _, n = scales.shape
    words = np.ascontiguousarray(words).reshape(g, 128, n, 2)
    nib = np.empty((g, 128, n, 4), np.uint8)
    nib[..., 0::2] = words & 0xF
    nib[..., 1::2] = words >> 4
    vals = E2M1[nib] * np.repeat(np.exp2(scales.astype(np.float64) - 127.0), 8, axis=1)[..., None]
    return vals.transpose(0, 1, 3, 2).reshape(g * 512, n)


def sigmoid(v):
    return 1.0 / (1.0 + np.exp(-np.maximum(v, -700.0)))

def planes(y):
    n, m = y.shape
    v = y.astype(np.float32).astype(ml_dtypes.bfloat16).astype(np.float64).reshape(n // 32, 32, m)
    top = np.abs(v).max(1)
    byte = np.clip(np.where(top > 0, np.frexp(top)[1] - 1 + 127 - 7, 1), 1, 254)
    codes = (v * np.exp2(127.0 - byte)[:, None, :]).reshape(n, m).astype(np.float32).astype(ml_dtypes.float8_e4m3fn).view(np.uint8)
    words = codes.reshape(n // 512, 128, 4, m).transpose(0, 1, 3, 2)
    return np.ascontiguousarray(words), np.ascontiguousarray(byte.astype(np.uint8).reshape(n // 512, 16, m))


K, T, S, H = 512, 2048, 512, 512


def setup_inputs():
    n = np.random.standard_normal
    s = mx_kscale(K)[:, None]
    u = mx_kscale(H)
    packed_xT = pack_weight(n((K, T)) * s)
    packed_w1 = pack_fp4(n((K, H)) / np.sqrt(K) / s)
    packed_w2 = pack_fp4(n((H, H)) / np.sqrt(H) / u[:, None])
    return {
        "x_words": packed_xT[0],
        "x_scales": packed_xT[1],
        "w1_words": packed_w1[0],
        "w1_scales": packed_w1[1],
        "gn": (np.random.uniform(0.5, 1.5, (H, 1)) * u[:, None]).astype(np.float32),
        "w2_words": packed_w2[0],
        "w2_scales": packed_w2[1],
        "offs": striped(np.random.permutation(T)[:S]),
        "n1": striped8(np.stack([np.random.permutation(S) for _ in range(8)])),
        "n2": striped8(np.stack([np.random.permutation(S) for _ in range(8)])),
        "n3": striped8(np.stack([np.random.permutation(S) for _ in range(8)])),
        "n4": striped8(np.stack([np.random.permutation(S) for _ in range(8)])),
        "n5": striped8(np.stack([np.random.permutation(S) for _ in range(8)])),
        "n6": striped8(np.stack([np.random.permutation(S) for _ in range(8)])),
        "n7": striped8(np.stack([np.random.permutation(S) for _ in range(8)])),
    }


def reference(x_words, x_scales, w1_words, w1_scales, gn, w2_words, w2_scales, offs, n1, n2, n3, n4, n5, n6, n7):
    xq = unpack_weight(x_words, x_scales)[:, unstriped(offs)]
    y = unpack_fp4(w1_words, w1_scales).T @ xq
    pa = y[np.arange(H)[:, None], runs(n1, H)]
    pb = y[np.arange(H)[:, None], runs(n2, H)]
    z = f64(gn) * (np.maximum(np.minimum(y, pa), np.minimum(np.maximum(y, pa), pb)))
    w2q = unpack_fp4(w2_words, w2_scales)
    a = w2q.T @ mxq(z, 0, "e4m3")
    pa2 = y[np.arange(H)[:, None], runs(n3, H)]
    z2 = f64(gn) * (pa2 + (sigmoid(y[np.arange(H)[:, None], runs(n4, H)])) * (y[np.arange(H)[:, None], runs(n5, H)] - pa2))
    b = w2q.T @ mxq(z2, 0, "e4m3")
    out_0 = a + (sigmoid(b[np.arange(H)[:, None], runs(n7, H)] - b)) * (a[np.arange(H)[:, None], runs(n6, H)] - a)
    return (out_0,) + planes(out_0)

@@ -1,0 +1,262 @@
+from contextlib import ExitStack
+
+import concourse.mybir as mybir
+from concourse.masks import make_identity
+
+K, T, S, H = 512, 2048, 512, 512
+FLOPS = 3 * 2 * 512 * 512 * 512
+
+F32 = mybir.dt.float32
+BF16 = mybir.dt.bfloat16
+I32 = mybir.dt.int32
+U32 = mybir.dt.uint32
+U16 = mybir.dt.uint16
+U8 = mybir.dt.uint8
+FP8X4 = mybir.dt.float8_e4m3fn_x4
+FP4X4 = mybir.dt.float4_e2m1fn_x4
+ALU = mybir.AluOpType
+ACT = mybir.ActivationFunctionType
+
+P = 128
+PACK = 4
+HALF = S // 2
+WIDE = 2 * S
+
+
+def tile_picked_tiepullbmedlerp_none_po_kernel(
+    tc, x_words, x_scales, w1_words, w1_scales, gn, w2_words, w2_scales,
+    offs, n1, n2, n3, n4, n5, n6, n7, out_0, out_1, out_2,
+):
+    nc = tc.nc
+    with ExitStack() as ctx:
+        lists = ctx.enter_context(tc.tile_pool(name="lists", bufs=1))
+        sb = ctx.enter_context(tc.tile_pool(name="sb", bufs=1))
+        ps = ctx.enter_context(tc.psum_pool(name="ps", bufs=1))
+
+        def load_list(name, src):
+            tile = lists.tile([P, S // 16], U16, name=name)
+            nc.sync.dma_start(tile[:], src)
+            return tile
+
+        def bank(number, name, shape):
+            return ps.tile(shape, F32, name=name, tag="bank%d" % number)
+
+        def zeroed_plane(engine, name, width):
+            plane = sb.tile([P, width], U8, name=name, align_bytes=64)
+            engine.memset(plane[:].bitcast(I32), 0)
+            return plane
+
+        def load_scale_rows(queues, plane, src):
+            for q in range(4):
+                queues[q].dma_start(plane[32 * q : 32 * q + 4, :].bitcast(I32), src[0, 4 * q : 4 * q + 4, :].bitcast(I32))
+
+        def deal_weights(name, words, plane, words_tag, plane_tag):
+            dealt_words = sb.tile([P, PACK, 2 * P], U8, name=name + "_dealt_words", tag=words_tag, align_bytes=64)
+            dealt_plane = sb.tile([P, PACK, P], U8, name=name + "_dealt_plane", tag=plane_tag, align_bytes=64)
+            nc.vector.tensor_copy(
+                dealt_words[:].rearrange("p t (m b) -> p t m b", b=2),
+                words[:].rearrange("p (m t b) -> p t m b", t=PACK, b=2),
+            )
+            nc.vector.tensor_copy(dealt_plane[:], plane[:].rearrange("p (m t) -> p t m", t=PACK))
+            return dealt_words, dealt_plane
+
+        def product(acc, weights, t, codes, plane):
+            nc.tensor.matmul_mx(
+                out=acc, lhsT=weights[0][:, t, :].bitcast(FP4X4), lhsT_scale=weights[1][:, t, :],
+                rhs=codes.bitcast(FP8X4), rhs_scale=plane, start=True, stop=True,
+            )
+
+        w1_plane = zeroed_plane(nc.gpsimd, "w1_plane", H)
+        x_plane = zeroed_plane(nc.vector, "x_plane", T)
+        offs_sb = load_list("offs_sb", offs)
+        w1_sb = sb.tile([P, 2 * H], U8, name="w1_sb")
+        nc.sync.dma_start(w1_sb[96:, :].bitcast(I32), w1_words[0, 96:, :].bitcast(I32))
+        x_sb = sb.tile([P, T], U32, name="x_sb")
+        nc.sync.dma_start(x_sb[:].bitcast(I32), x_words[0].rearrange("p c r -> p (c r)").bitcast(I32))
+        nc.sync.dma_start(w1_sb[:96, :].bitcast(I32), w1_words[0, :96, :].bitcast(I32))
+        load_scale_rows([nc.sync] * 4, x_plane, x_scales)
+        load_scale_rows([nc.gpsimd, nc.gpsimd, nc.sync, nc.sync], w1_plane, w1_scales)
+        gain = sb.tile([P, PACK], F32, name="gain")
+        nc.gpsimd.dma_start(gain[:], gn.rearrange("(p t) o -> p (t o)", t=PACK))
+        w2_plane = zeroed_plane(nc.gpsimd, "w2_plane", H)
+        n4_sb = load_list("n4_sb", n4)
+        n1_sb = load_list("n1_sb", n1)
+        n2_sb = load_list("n2_sb", n2)
+        n5_sb = load_list("n5_sb", n5)
+        n3_sb = load_list("n3_sb", n3)
+        w2_sb = sb.tile([P, 2 * H], U8, name="w2_sb")
+        nc.sync.dma_start(w2_sb[:].bitcast(I32), w2_words[0].bitcast(I32))
+        load_scale_rows([nc.sync] * 4, w2_plane, w2_scales)
+        n7_sb = load_list("n7_sb", n7)
+        n6_sb = load_list("n6_sb", n6)
+        ident = sb.tile([P, P], F32, name="ident")
+        make_identity(nc, ident[:])
+
+        picked_plane = sb.tile([P, S], U8, name="picked_plane", align_bytes=64)
+        nc.vector.tensor_copy(picked_plane[:], x_plane[:].indirect(offs_sb[:]))
+        w1 = deal_weights("w1", w1_sb, w1_plane, "w1_dealt_words", "w1_dealt_plane")
+        picked = sb.tile([P, S], U32, name="picked", align_bytes=64)
+        nc.vector.tensor_copy(picked[:], x_sb[:].indirect(offs_sb[:]))
+
+        def add_turned(acc, term, first, last):
+            nc.tensor.matmul(acc, lhsT=term, rhs=ident[:], is_transpose=True, start=first, stop=last)
+
+        def round_and_pair(name, sums):
+            paired = sb.tile([P, 2, P, 2], BF16, name=name)
+            nc.scalar.copy(paired[:], sums[:].rearrange("c (u e) p -> c u p e", e=2))
+            return paired
+
+        def turn_back(acc, paired, chunk):
+            words = paired[:].rearrange("c u p e -> c (u p e)").bitcast(F32)
+            for u in range(2):
+                nc.tensor.transpose(acc[:, u, chunk * P : (chunk + 1) * P], words[:, u * P : (u + 1) * P], ident[:])
+
+        def quantise_half(name, acc, codes, plane):
+            grouped = sb.tile([P, HALF * PACK], BF16, name=name, align_bytes=64)
+            nc.scalar.copy(grouped[:].bitcast(F32).rearrange("p (c u) -> p c u", u=2), acc[:].rearrange("p u c -> p c u"))
+            nc.vector.quantize_mx(out=codes.bitcast(FP8X4), scales=plane, in_=grouped[:])
+
+        gate = sb.tile([P, PACK, S], F32, name="gate")
+        rest = sb.tile([P, PACK, S], F32, name="rest")
+        far = sb.tile([P, PACK, S], F32, name="far")
+        near = sb.tile([P, PACK, S], F32, name="near")
+        d1 = sb.tile([P, PACK, S], F32, name="d1")
+        d2 = sb.tile([P, PACK, S], F32, name="d2")
+        upper = sb.tile([P, PACK, S], F32, name="upper")
+        z2_sums = [bank(1 + c, "z2_sums%d" % c, [P, PACK, P]) for c in range(4)]
+        gy = []
+        gy_plain = []
+
+        def pulls(t):
+            nc.vector.tensor_tensor(d1[:, t, :], gy[t][:].indirect(n1_sb[:]), gy_plain[t], ALU.subtract)
+            nc.vector.tensor_tensor(d2[:, t, :], gy[t][:].indirect(n2_sb[:]), gy_plain[t], ALU.subtract)
+
+        def upper_clamp(t):
+            nc.vector.scalar_tensor_tensor(upper[:, t, :], d1[:, t, :], 0.0, d2[:, t, :], ALU.max, ALU.min)
+
+        for t in range(PACK):
+            y_acc = bank(0, "y_acc%d" % t, [P, S])
+            product(y_acc[:], w1, t, picked[:], picked_plane[:])
+            y = sb.tile([P, WIDE], F32, name="y%d" % t, tag="y%d" % t, align_bytes=64)
+            gy.append(sb.tile([P, WIDE], F32, name="gy%d" % t))
+            if t == 0:
+                first_plain = sb.tile([P, S], F32, name="first_plain", tag="first_plain", align_bytes=64)
+                nc.vector.tensor_copy(y[:, :S], y_acc[:])
+                nc.vector.tensor_scalar_mul(gy[0][:, :S], y[:, :S], gain[:, 0:1])
+                nc.vector.tensor_scalar_mul(first_plain[:], y[:, :S], gain[:, 0:1])
+                gy_plain.append(first_plain[:])
+            else:
+                nc.scalar.copy(y[:, :S], y_acc[:])
+                nc.scalar.activation(gy[t][:, :S], y_acc[:], ACT.Copy, scale=gain[:, t : t + 1])
+            nc.scalar.activation(gate[:, t, :], y[:].indirect(n4_sb[:]), ACT.Sigmoid)
+            nc.scalar.activation(rest[:, t, :], gate[:, t, :], ACT.Copy, bias=1.0, scale=-1.0)
+            if t == 0:
+                pulls(0)
+            nc.vector.tensor_tensor(far[:, t, :], gy[t][:].indirect(n5_sb[:]), gate[:, t, :], ALU.mult)
+            nc.vector.tensor_tensor(near[:, t, :], gy[t][:].indirect(n3_sb[:]), rest[:, t, :], ALU.mult)
+            for c in range(4):
+                cols = slice(c * P, (c + 1) * P)
+                add_turned(z2_sums[c][:, t, :], far[:, t, cols], True, False)
+                add_turned(z2_sums[c][:, t, :], near[:, t, cols], False, True)
+
+        w2 = deal_weights("w2", w2_sb, w2_plane, "first_plain", "y1")
+        later_plain = sb.tile([P, PACK - 1, S], F32, name="later_plain", tag="y3", align_bytes=64)
+        for t in range(1, PACK):
+            nc.scalar.copy(later_plain[:, t - 1, :], gy[t][:, :S])
+            gy_plain.append(later_plain[:, t - 1, :])
+
+        z2_codes = sb.tile([P, S], U32, name="z2_codes", align_bytes=64)
+        z2_plane = sb.tile([P, S], U8, name="z2_plane", align_bytes=64)
+        for h in range(2):
+            acc = bank(5 + h, "z2_back%d" % h, [P, 2, HALF])
+            for i in range(2):
+                turn_back(acc, round_and_pair("z2_paired%d" % (2 * h + i), z2_sums[2 * h + i]), i)
+            cols = slice(h * HALF, (h + 1) * HALF)
+            quantise_half("z2_grouped%d" % h, acc, z2_codes[:, cols], z2_plane[:, cols])
+        b = []
+        b_plain = sb.tile([P, PACK, S], F32, name="b_plain")
+        for t in range(PACK):
+            b_acc = bank((7, 0, 1, 2)[t], "b_acc%d" % t, [P, S])
+            product(b_acc[:], w2, t, z2_codes[:], z2_plane[:])
+            b.append(sb.tile([P, WIDE], F32, name="b%d" % t))
+            nc.scalar.copy(b[t][:, :S], b_acc[:])
+            nc.scalar.copy(b_plain[:, t, :], b_acc[:])
+
+        for t in range(1, PACK):
+            pulls(t)
+            upper_clamp(t - 1)
+        upper_clamp(PACK - 1)
+        z_sums = [bank(3 + c, "z_sums%d" % c, [P, PACK, P]) for c in range(4)]
+        for c in range(4):
+            for t in range(PACK):
+                add_turned(z_sums[c][:, t, :], gy[t][:, c * P : (c + 1) * P], t == 0, False)
+        a_acc = [bank(1 + t, "a_acc%d" % t, [P, S]) for t in range(PACK)]
+        mix = sb.tile([P, PACK, S], F32, name="mix")
+        for h in range(2):
+            cols = slice(h * HALF, (h + 1) * HALF)
+            pull = sb.tile([P, PACK, HALF], F32, name="pull%d" % h)
+            nc.vector.scalar_tensor_tensor(pull[:], d1[:, :, cols], 0.0, upper[:, :, cols], ALU.min, ALU.max)
+            acc = bank((7, 0)[h], "z_back%d" % h, [P, 2, HALF])
+            for i in range(2):
+                c = 2 * h + i
+                for t in range(PACK):
+                    add_turned(z_sums[c][:, t, :], pull[:, t, i * P : (i + 1) * P], False, t == PACK - 1)
+                turn_back(acc, round_and_pair("z_paired%d" % c, z_sums[c]), i)
+            z_codes = sb.tile([P, HALF], U32, name="z_codes%d" % h, align_bytes=64)
+            z_plane = sb.tile([P, HALF], U8, name="z_plane%d" % h, align_bytes=64)
+            quantise_half("z_grouped%d" % h, acc, z_codes[:], z_plane[:])
+            for t in range(PACK):
+                product(a_acc[t][:, cols], w2, t, z_codes[:], z_plane[:])
+        for t in range(PACK):
+            nc.vector.tensor_tensor(mix[:, t, :], b[t][:].indirect(n7_sb[:]), b_plain[:, t, :], ALU.subtract)
+            nc.scalar.activation(mix[:, t, :], mix[:, t, :], ACT.Sigmoid)
+
+        a = []
+        kept = sb.tile([P, PACK, S], F32, name="kept")
+        drawn = [sb.tile([P, PACK, HALF], F32, name="drawn%d" % h) for h in range(2)]
+
+        def draw(t, h):
+            nc.vector.tensor_tensor(
+                drawn[h][:, t, :], a[t][:].indirect(n6_sb[:, h * 16 : (h + 1) * 16]),
+                mix[:, t, h * HALF : (h + 1) * HALF], ALU.mult,
+            )
+
+        out_rows = out_0.rearrange("(p t) c -> p t c", t=PACK)
+        out_words = out_1[0].rearrange("p c r -> p (c r)").bitcast(I32)
+        out_codes = sb.tile([P, S], U32, name="out_codes", align_bytes=64)
+        out_plane = sb.tile([P, S], U8, name="out_plane", align_bytes=64)
+
+        def finish(lo, hi):
+            h = lo // HALF
+            result = sb.tile([P, PACK, hi - lo], F32, name="result%d" % lo)
+            nc.vector.tensor_tensor(result[:], drawn[h][:, :, lo - h * HALF : hi - h * HALF], kept[:, :, lo:hi], ALU.subtract)
+            nc.sync.dma_start(out_rows[:, :, lo:hi], result[:])
+            grouped = sb.tile([P, hi - lo, PACK], BF16, name="out_grouped%d" % lo, align_bytes=64)
+            nc.scalar.copy(
+                grouped[:].rearrange("p (c i) t -> p c t i", i=4), result[:].rearrange("p t (c i) -> p c t i", i=4)
+            )
+            return grouped
+
+        def hand_on(lo, hi, grouped):
+            nc.vector.quantize_mx(
+                out=out_codes[:, lo:hi].bitcast(FP8X4), scales=out_plane[:, lo:hi],
+                in_=grouped[:].rearrange("p c t -> p (c t)"),
+            )
+            nc.sync.dma_start(out_words[:, lo:hi], out_codes[:, lo:hi].bitcast(I32))
+
+        for t in range(PACK):
+            a.append(sb.tile([P, S], F32, name="a%d" % t))
+            nc.scalar.copy(a[t][:], a_acc[t][:])
+            draw(t, 0)
+            nc.vector.scalar_tensor_tensor(kept[:, t, :], mix[:, t, :], 1.0, a[t][:], ALU.subtract, ALU.mult)
+        g0 = finish(0, 256)
+        for t in range(PACK):
+            draw(t, 1)
+        g1 = finish(256, 384)
+        hand_on(0, 256, g0)
+        g2 = finish(384, 512)
+        hand_on(256, 384, g1)
+        hand_on(384, 512, g2)
+        for q in range(4):
+            queue = nc.scalar if q % 2 == 0 else nc.sync
+            queue.dma_start(out_2[0, 4 * q : 4 * q + 4, :].bitcast(I32), out_plane[32 * q : 32 * q + 4, :].bitcast(I32))

@@ -42,7 +42,7 @@ def tile_picked_tiepullbmedlerp_none_po_kernel(
             return ps.tile(shape, F32, name=name, tag="bank%d" % number)
 
         def zeroed_plane(engine, name, width):
-            plane = sb.tile([P, width], U8, name=name, align_bytes=64)
+            plane = sb.tile([P, width], U8, name=name, tag=name, align_bytes=64)
             engine.memset(plane[:].bitcast(I32), 0)
             return plane
 
@@ -50,15 +50,20 @@ def tile_picked_tiepullbmedlerp_none_po_kernel(
             for q in range(4):
                 queues[q].dma_start(plane[32 * q : 32 * q + 4, :].bitcast(I32), src[0, 4 * q : 4 * q + 4, :].bitcast(I32))
 
-        def deal_weights(name, words, plane, words_tag, plane_tag):
-            dealt_words = sb.tile([P, PACK, 2 * P], U8, name=name + "_dealt_words", tag=words_tag, align_bytes=64)
-            dealt_plane = sb.tile([P, PACK, P], U8, name=name + "_dealt_plane", tag=plane_tag, align_bytes=64)
-            nc.vector.tensor_copy(
-                dealt_words[:].rearrange("p t (m b) -> p t m b", b=2),
-                words[:].rearrange("p (m t b) -> p t m b", t=PACK, b=2),
-            )
-            nc.vector.tensor_copy(dealt_plane[:], plane[:].rearrange("p (m t) -> p t m", t=PACK))
-            return dealt_words, dealt_plane
+        def deal_words(name, words, tag, pieces):
+            dealt = sb.tile([P, PACK, 2 * P], U8, name=name, tag=tag, align_bytes=64)
+            step = PACK // pieces
+            for t in range(0, PACK, step):
+                nc.vector.tensor_copy(
+                    dealt[:, t : t + step, :].rearrange("p t (m b) -> p t m b", b=2),
+                    words[:].rearrange("p (m t b) -> p t m b", t=PACK, b=2)[:, t : t + step],
+                )
+            return dealt
+
+        def deal_plane(name, plane, tag):
+            dealt = sb.tile([P, PACK, P], U8, name=name, tag=tag, align_bytes=64)
+            nc.vector.tensor_copy(dealt[:], plane[:].rearrange("p (m t) -> p t m", t=PACK))
+            return dealt
 
         def product(acc, weights, t, codes, plane):
             nc.tensor.matmul_mx(
@@ -66,43 +71,44 @@ def tile_picked_tiepullbmedlerp_none_po_kernel(
                 rhs=codes.bitcast(FP8X4), rhs_scale=plane, start=True, stop=True,
             )
 
-        w1_plane = zeroed_plane(nc.gpsimd, "w1_plane", H)
         x_plane = zeroed_plane(nc.vector, "x_plane", T)
+        w1_plane = zeroed_plane(nc.gpsimd, "w1_plane", H)
         offs_sb = load_list("offs_sb", offs)
         w1_sb = sb.tile([P, 2 * H], U8, name="w1_sb")
-        nc.sync.dma_start(w1_sb[96:, :].bitcast(I32), w1_words[0, 96:, :].bitcast(I32))
-        x_sb = sb.tile([P, T], U32, name="x_sb")
+        nc.sync.dma_start(w1_sb[:].bitcast(I32), w1_words[0].bitcast(I32))
+        x_sb = sb.tile([P, T], U32, name="x_sb", tag="x_sb", align_bytes=64)
         nc.sync.dma_start(x_sb[:].bitcast(I32), x_words[0].rearrange("p c r -> p (c r)").bitcast(I32))
-        nc.sync.dma_start(w1_sb[:96, :].bitcast(I32), w1_words[0, :96, :].bitcast(I32))
+        w2_sb = sb.tile([P, 2 * H], U8, name="w2_sb")
+        nc.sync.dma_start(w2_sb[:96, :].bitcast(I32), w2_words[0, :96, :].bitcast(I32))
         load_scale_rows([nc.sync] * 4, x_plane, x_scales)
         load_scale_rows([nc.gpsimd, nc.gpsimd, nc.sync, nc.sync], w1_plane, w1_scales)
         gain = sb.tile([P, PACK], F32, name="gain")
         nc.gpsimd.dma_start(gain[:], gn.rearrange("(p t) o -> p (t o)", t=PACK))
         w2_plane = zeroed_plane(nc.gpsimd, "w2_plane", H)
         n4_sb = load_list("n4_sb", n4)
+        nc.sync.dma_start(w2_sb[96:, :].bitcast(I32), w2_words[0, 96:, :].bitcast(I32))
         n1_sb = load_list("n1_sb", n1)
         n2_sb = load_list("n2_sb", n2)
         n5_sb = load_list("n5_sb", n5)
         n3_sb = load_list("n3_sb", n3)
-        w2_sb = sb.tile([P, 2 * H], U8, name="w2_sb")
-        nc.sync.dma_start(w2_sb[:].bitcast(I32), w2_words[0].bitcast(I32))
         load_scale_rows([nc.sync] * 4, w2_plane, w2_scales)
         n7_sb = load_list("n7_sb", n7)
         n6_sb = load_list("n6_sb", n6)
         ident = sb.tile([P, P], F32, name="ident")
         make_identity(nc, ident[:])
 
-        picked_plane = sb.tile([P, S], U8, name="picked_plane", align_bytes=64)
-        nc.vector.tensor_copy(picked_plane[:], x_plane[:].indirect(offs_sb[:]))
-        w1 = deal_weights("w1", w1_sb, w1_plane, "w1_dealt_words", "w1_dealt_plane")
+        w1_dealt_words = deal_words("w1_dealt_words", w1_sb, "w1_dealt_words", 1)
         picked = sb.tile([P, S], U32, name="picked", align_bytes=64)
         nc.vector.tensor_copy(picked[:], x_sb[:].indirect(offs_sb[:]))
+        picked_plane = sb.tile([P, S], U8, name="picked_plane", tag="x_sb", align_bytes=64)
+        nc.vector.tensor_copy(picked_plane[:], x_plane[:].indirect(offs_sb[:]))
+        w1 = (w1_dealt_words, deal_plane("w1_dealt_plane", w1_plane, "w1_dealt_plane"))
 
         def add_turned(acc, term, first, last):
             nc.tensor.matmul(acc, lhsT=term, rhs=ident[:], is_transpose=True, start=first, stop=last)
 
         def round_and_pair(name, sums):
-            paired = sb.tile([P, 2, P, 2], BF16, name=name)
+            paired = sb.tile([P, 2, P, 2], BF16, name=name, tag=name, align_bytes=64)
             nc.scalar.copy(paired[:], sums[:].rearrange("c (u e) p -> c u p e", e=2))
             return paired
 
@@ -112,7 +118,7 @@ def tile_picked_tiepullbmedlerp_none_po_kernel(
                 nc.tensor.transpose(acc[:, u, chunk * P : (chunk + 1) * P], words[:, u * P : (u + 1) * P], ident[:])
 
         def quantise_half(name, acc, codes, plane):
-            grouped = sb.tile([P, HALF * PACK], BF16, name=name, align_bytes=64)
+            grouped = sb.tile([P, HALF * PACK], BF16, name=name, tag=name, align_bytes=64)
             nc.scalar.copy(grouped[:].bitcast(F32).rearrange("p (c u) -> p c u", u=2), acc[:].rearrange("p u c -> p c u"))
             nc.vector.quantize_mx(out=codes.bitcast(FP8X4), scales=plane, in_=grouped[:])
 
@@ -131,8 +137,13 @@ def tile_picked_tiepullbmedlerp_none_po_kernel(
             nc.vector.tensor_tensor(d1[:, t, :], gy[t][:].indirect(n1_sb[:]), gy_plain[t], ALU.subtract)
             nc.vector.tensor_tensor(d2[:, t, :], gy[t][:].indirect(n2_sb[:]), gy_plain[t], ALU.subtract)
 
-        def upper_clamp(t):
-            nc.vector.scalar_tensor_tensor(upper[:, t, :], d1[:, t, :], 0.0, d2[:, t, :], ALU.max, ALU.min)
+        def upper_clamp(t, cols):
+            nc.vector.scalar_tensor_tensor(upper[:, t, cols], d1[:, t, cols], 0.0, d2[:, t, cols], ALU.max, ALU.min)
+
+        def plain_copy(t, tag):
+            plain = sb.tile([P, S], F32, name="gy_plain%d" % t, tag=tag, align_bytes=64)
+            nc.scalar.copy(plain[:], gy[t][:, :S])
+            gy_plain.append(plain[:])
 
         for t in range(PACK):
             y_acc = bank(0, "y_acc%d" % t, [P, S])
@@ -159,11 +170,10 @@ def tile_picked_tiepullbmedlerp_none_po_kernel(
                 add_turned(z2_sums[c][:, t, :], far[:, t, cols], True, False)
                 add_turned(z2_sums[c][:, t, :], near[:, t, cols], False, True)
 
-        w2 = deal_weights("w2", w2_sb, w2_plane, "first_plain", "y1")
-        later_plain = sb.tile([P, PACK - 1, S], F32, name="later_plain", tag="y3", align_bytes=64)
-        for t in range(1, PACK):
-            nc.scalar.copy(later_plain[:, t - 1, :], gy[t][:, :S])
-            gy_plain.append(later_plain[:, t - 1, :])
+        w2 = (deal_words("w2_dealt_words", w2_sb, "x_plane", 2), deal_plane("w2_dealt_plane", w2_plane, "y1"))
+        plain_copy(1, "y3")
+        pulls(1)
+        upper_clamp(0, slice(0, S))
 
         z2_codes = sb.tile([P, S], U32, name="z2_codes", align_bytes=64)
         z2_plane = sb.tile([P, S], U8, name="z2_plane", align_bytes=64)
@@ -173,6 +183,9 @@ def tile_picked_tiepullbmedlerp_none_po_kernel(
                 turn_back(acc, round_and_pair("z2_paired%d" % (2 * h + i), z2_sums[2 * h + i]), i)
             cols = slice(h * HALF, (h + 1) * HALF)
             quantise_half("z2_grouped%d" % h, acc, z2_codes[:, cols], z2_plane[:, cols])
+            plain_copy(2 + h, "z2_paired%d" % (2 * h + 1))
+            pulls(2 + h)
+            upper_clamp(1 + h, slice(0, S))
         b = []
         b_plain = sb.tile([P, PACK, S], F32, name="b_plain")
         for t in range(PACK):
@@ -182,16 +195,14 @@ def tile_picked_tiepullbmedlerp_none_po_kernel(
             nc.scalar.copy(b[t][:, :S], b_acc[:])
             nc.scalar.copy(b_plain[:, t, :], b_acc[:])
 
-        for t in range(1, PACK):
-            pulls(t)
-            upper_clamp(t - 1)
-        upper_clamp(PACK - 1)
+        for h in range(2):
+            upper_clamp(PACK - 1, slice(h * HALF, (h + 1) * HALF))
         z_sums = [bank(3 + c, "z_sums%d" % c, [P, PACK, P]) for c in range(4)]
         for c in range(4):
             for t in range(PACK):
                 add_turned(z_sums[c][:, t, :], gy[t][:, c * P : (c + 1) * P], t == 0, False)
         a_acc = [bank(1 + t, "a_acc%d" % t, [P, S]) for t in range(PACK)]
-        mix = sb.tile([P, PACK, S], F32, name="mix")
+        mix = []
         for h in range(2):
             cols = slice(h * HALF, (h + 1) * HALF)
             pull = sb.tile([P, PACK, HALF], F32, name="pull%d" % h)
@@ -208,8 +219,10 @@ def tile_picked_tiepullbmedlerp_none_po_kernel(
             for t in range(PACK):
                 product(a_acc[t][:, cols], w2, t, z_codes[:], z_plane[:])
         for t in range(PACK):
-            nc.vector.tensor_tensor(mix[:, t, :], b[t][:].indirect(n7_sb[:]), b_plain[:, t, :], ALU.subtract)
-            nc.scalar.activation(mix[:, t, :], mix[:, t, :], ACT.Sigmoid)
+            tag = ("mix0", "mix1", "z_grouped0", "z_grouped1")[t]
+            mix.append(sb.tile([P, S], F32, name="mix%d" % t, tag=tag, align_bytes=64))
+            nc.vector.tensor_tensor(mix[t][:], b[t][:].indirect(n7_sb[:]), b_plain[:, t, :], ALU.subtract)
+            nc.scalar.activation(mix[t][:], mix[t][:], ACT.Sigmoid)
 
         a = []
         kept = sb.tile([P, PACK, S], F32, name="kept")
@@ -218,7 +231,7 @@ def tile_picked_tiepullbmedlerp_none_po_kernel(
         def draw(t, h):
             nc.vector.tensor_tensor(
                 drawn[h][:, t, :], a[t][:].indirect(n6_sb[:, h * 16 : (h + 1) * 16]),
-                mix[:, t, h * HALF : (h + 1) * HALF], ALU.mult,
+                mix[t][:, h * HALF : (h + 1) * HALF], ALU.mult,
             )
 
         out_rows = out_0.rearrange("(p t) c -> p t c", t=PACK)
@@ -248,7 +261,7 @@ def tile_picked_tiepullbmedlerp_none_po_kernel(
             a.append(sb.tile([P, S], F32, name="a%d" % t))
             nc.scalar.copy(a[t][:], a_acc[t][:])
             draw(t, 0)
-            nc.vector.scalar_tensor_tensor(kept[:, t, :], mix[:, t, :], 1.0, a[t][:], ALU.subtract, ALU.mult)
+            nc.vector.scalar_tensor_tensor(kept[:, t, :], mix[t][:], 1.0, a[t][:], ALU.subtract, ALU.mult)
         g0 = finish(0, 256)
         for t in range(PACK):
             draw(t, 1)

@@ -82,10 +82,10 @@ def tile_picked_tiepullbmedlerp_none_po_kernel(
         nc.sync.dma_start(w2_sb[:96, :].bitcast(I32), w2_words[0, :96, :].bitcast(I32))
         load_scale_rows([nc.sync] * 4, x_plane, x_scales)
         load_scale_rows([nc.gpsimd, nc.gpsimd, nc.sync, nc.sync], w1_plane, w1_scales)
-        gain = sb.tile([P, PACK], F32, name="gain")
-        nc.gpsimd.dma_start(gain[:], gn.rearrange("(p t) o -> p (t o)", t=PACK))
-        w2_plane = zeroed_plane(nc.gpsimd, "w2_plane", H)
+        w2_plane = zeroed_plane(nc.vector, "w2_plane", H)
         n4_sb = load_list("n4_sb", n4)
+        gain = sb.tile([P, PACK], F32, name="gain")
+        nc.sync.dma_start(gain[:], gn.rearrange("(p t) o -> p (t o)", t=PACK))
         nc.sync.dma_start(w2_sb[96:, :].bitcast(I32), w2_words[0, 96:, :].bitcast(I32))
         n1_sb = load_list("n1_sb", n1)
         n2_sb = load_list("n2_sb", n2)
@@ -95,13 +95,16 @@ def tile_picked_tiepullbmedlerp_none_po_kernel(
         n7_sb = load_list("n7_sb", n7)
         n6_sb = load_list("n6_sb", n6)
         ident = sb.tile([P, P], F32, name="ident")
-        make_identity(nc, ident[:])
+        nc.vector.memset(ident[:], 0.0)
+        warm = sb.tile([P, 1], F32, name="warm")
+        nc.scalar.activation(warm[:], ident[:, 0:1], ACT.Sigmoid)
+        make_identity(nc, ident[:], nomemset=True)
 
         w1_dealt_words = deal_words("w1_dealt_words", w1_sb, "w1_dealt_words", 1)
+        picked_plane = sb.tile([P, S], U8, name="picked_plane", align_bytes=64)
+        nc.vector.tensor_copy(picked_plane[:], x_plane[:].indirect(offs_sb[:]))
         picked = sb.tile([P, S], U32, name="picked", align_bytes=64)
         nc.vector.tensor_copy(picked[:], x_sb[:].indirect(offs_sb[:]))
-        picked_plane = sb.tile([P, S], U8, name="picked_plane", tag="x_sb", align_bytes=64)
-        nc.vector.tensor_copy(picked_plane[:], x_plane[:].indirect(offs_sb[:]))
         w1 = (w1_dealt_words, deal_plane("w1_dealt_plane", w1_plane, "w1_dealt_plane"))
 
         def add_turned(acc, term, first, last):
@@ -129,7 +132,7 @@ def tile_picked_tiepullbmedlerp_none_po_kernel(
         d1 = sb.tile([P, PACK, S], F32, name="d1")
         d2 = sb.tile([P, PACK, S], F32, name="d2")
         upper = sb.tile([P, PACK, S], F32, name="upper")
-        z2_sums = [bank(1 + c, "z2_sums%d" % c, [P, PACK, P]) for c in range(4)]
+        z2_sums = [bank(4 + c, "z2_sums%d" % c, [P, PACK, P]) for c in range(4)]
         gy = []
         gy_plain = []
 
@@ -146,19 +149,16 @@ def tile_picked_tiepullbmedlerp_none_po_kernel(
             gy_plain.append(plain[:])
 
         for t in range(PACK):
-            y_acc = bank(0, "y_acc%d" % t, [P, S])
+            y_acc = bank(t, "y_acc%d" % t, [P, S])
             product(y_acc[:], w1, t, picked[:], picked_plane[:])
             y = sb.tile([P, WIDE], F32, name="y%d" % t, tag="y%d" % t, align_bytes=64)
             gy.append(sb.tile([P, WIDE], F32, name="gy%d" % t))
+            nc.scalar.activation(gy[t][:, :S], y_acc[:], ACT.Copy, scale=gain[:, t : t + 1])
+            nc.scalar.copy(y[:, :S], y_acc[:])
             if t == 0:
-                first_plain = sb.tile([P, S], F32, name="first_plain", tag="first_plain", align_bytes=64)
-                nc.vector.tensor_copy(y[:, :S], y_acc[:])
-                nc.vector.tensor_scalar_mul(gy[0][:, :S], y[:, :S], gain[:, 0:1])
-                nc.vector.tensor_scalar_mul(first_plain[:], y[:, :S], gain[:, 0:1])
+                first_plain = sb.tile([P, S], F32, name="first_plain")
+                nc.vector.tensor_copy(first_plain[:], gy[0][:, :S])
                 gy_plain.append(first_plain[:])
-            else:
-                nc.scalar.copy(y[:, :S], y_acc[:])
-                nc.scalar.activation(gy[t][:, :S], y_acc[:], ACT.Copy, scale=gain[:, t : t + 1])
             nc.scalar.activation(gate[:, t, :], y[:].indirect(n4_sb[:]), ACT.Sigmoid)
             nc.scalar.activation(rest[:, t, :], gate[:, t, :], ACT.Copy, bias=1.0, scale=-1.0)
             if t == 0:
@@ -170,7 +170,7 @@ def tile_picked_tiepullbmedlerp_none_po_kernel(
                 add_turned(z2_sums[c][:, t, :], far[:, t, cols], True, False)
                 add_turned(z2_sums[c][:, t, :], near[:, t, cols], False, True)
 
-        w2 = (deal_words("w2_dealt_words", w2_sb, "x_plane", 2), deal_plane("w2_dealt_plane", w2_plane, "y1"))
+        w2 = (deal_words("w2_dealt_words", w2_sb, "x_sb", 2), deal_plane("w2_dealt_plane", w2_plane, "y1"))
         plain_copy(1, "y3")
         pulls(1)
         upper_clamp(0, slice(0, S))
@@ -178,7 +178,7 @@ def tile_picked_tiepullbmedlerp_none_po_kernel(
         z2_codes = sb.tile([P, S], U32, name="z2_codes", align_bytes=64)
         z2_plane = sb.tile([P, S], U8, name="z2_plane", align_bytes=64)
         for h in range(2):
-            acc = bank(5 + h, "z2_back%d" % h, [P, 2, HALF])
+            acc = bank(h, "z2_back%d" % h, [P, 2, HALF])
             for i in range(2):
                 turn_back(acc, round_and_pair("z2_paired%d" % (2 * h + i), z2_sums[2 * h + i]), i)
             cols = slice(h * HALF, (h + 1) * HALF)
@@ -189,7 +189,7 @@ def tile_picked_tiepullbmedlerp_none_po_kernel(
         b = []
         b_plain = sb.tile([P, PACK, S], F32, name="b_plain")
         for t in range(PACK):
-            b_acc = bank((7, 0, 1, 2)[t], "b_acc%d" % t, [P, S])
+            b_acc = bank(2 + t, "b_acc%d" % t, [P, S])
             product(b_acc[:], w2, t, z2_codes[:], z2_plane[:])
             b.append(sb.tile([P, WIDE], F32, name="b%d" % t))
             nc.scalar.copy(b[t][:, :S], b_acc[:])
@@ -197,17 +197,17 @@ def tile_picked_tiepullbmedlerp_none_po_kernel(
 
         for h in range(2):
             upper_clamp(PACK - 1, slice(h * HALF, (h + 1) * HALF))
-        z_sums = [bank(3 + c, "z_sums%d" % c, [P, PACK, P]) for c in range(4)]
+        z_sums = [bank((6 + c) % 8, "z_sums%d" % c, [P, PACK, P]) for c in range(4)]
         for c in range(4):
             for t in range(PACK):
                 add_turned(z_sums[c][:, t, :], gy[t][:, c * P : (c + 1) * P], t == 0, False)
-        a_acc = [bank(1 + t, "a_acc%d" % t, [P, S]) for t in range(PACK)]
+        a_acc = [bank(4 + t, "a_acc%d" % t, [P, S]) for t in range(PACK)]
         mix = []
         for h in range(2):
             cols = slice(h * HALF, (h + 1) * HALF)
             pull = sb.tile([P, PACK, HALF], F32, name="pull%d" % h)
             nc.vector.scalar_tensor_tensor(pull[:], d1[:, :, cols], 0.0, upper[:, :, cols], ALU.min, ALU.max)
-            acc = bank((7, 0)[h], "z_back%d" % h, [P, 2, HALF])
+            acc = bank(2 + h, "z_back%d" % h, [P, 2, HALF])
             for i in range(2):
                 c = 2 * h + i
                 for t in range(PACK):

@@ -78,15 +78,14 @@ def tile_picked_tiepullbmedlerp_none_po_kernel(
         nc.sync.dma_start(w1_sb[:].bitcast(I32), w1_words[0].bitcast(I32))
         x_sb = sb.tile([P, T], U32, name="x_sb", tag="x_sb", align_bytes=64)
         nc.sync.dma_start(x_sb[:].bitcast(I32), x_words[0].rearrange("p c r -> p (c r)").bitcast(I32))
-        w2_sb = sb.tile([P, 2 * H], U8, name="w2_sb")
-        nc.sync.dma_start(w2_sb[:96, :].bitcast(I32), w2_words[0, :96, :].bitcast(I32))
+        gain = sb.tile([P, PACK], F32, name="gain")
+        nc.sync.dma_start(gain[:], gn.rearrange("(p t) o -> p (t o)", t=PACK))
         load_scale_rows([nc.sync] * 4, x_plane, x_scales)
         load_scale_rows([nc.gpsimd, nc.gpsimd, nc.sync, nc.sync], w1_plane, w1_scales)
         w2_plane = zeroed_plane(nc.vector, "w2_plane", H)
         n4_sb = load_list("n4_sb", n4)
-        gain = sb.tile([P, PACK], F32, name="gain")
-        nc.sync.dma_start(gain[:], gn.rearrange("(p t) o -> p (t o)", t=PACK))
-        nc.sync.dma_start(w2_sb[96:, :].bitcast(I32), w2_words[0, 96:, :].bitcast(I32))
+        w2_sb = sb.tile([P, 2 * H], U8, name="w2_sb")
+        nc.sync.dma_start(w2_sb[:].bitcast(I32), w2_words[0].bitcast(I32))
         n1_sb = load_list("n1_sb", n1)
         n2_sb = load_list("n2_sb", n2)
         n5_sb = load_list("n5_sb", n5)
@@ -143,10 +142,9 @@ def tile_picked_tiepullbmedlerp_none_po_kernel(
         def upper_clamp(t, cols):
             nc.vector.scalar_tensor_tensor(upper[:, t, cols], d1[:, t, cols], 0.0, d2[:, t, cols], ALU.max, ALU.min)
 
-        def plain_copy(t, tag):
-            plain = sb.tile([P, S], F32, name="gy_plain%d" % t, tag=tag, align_bytes=64)
-            nc.scalar.copy(plain[:], gy[t][:, :S])
-            gy_plain.append(plain[:])
+        def plain_copy(t, plain):
+            nc.scalar.copy(plain, gy[t][:, :S])
+            gy_plain.append(plain)
 
         for t in range(PACK):
             y_acc = bank(t, "y_acc%d" % t, [P, S])
@@ -171,9 +169,11 @@ def tile_picked_tiepullbmedlerp_none_po_kernel(
                 add_turned(z2_sums[c][:, t, :], near[:, t, cols], False, True)
 
         w2 = (deal_words("w2_dealt_words", w2_sb, "x_sb", 2), deal_plane("w2_dealt_plane", w2_plane, "y1"))
-        plain_copy(1, "y3")
-        pulls(1)
-        upper_clamp(0, slice(0, S))
+        middle_plain = sb.tile([P, 2, S], F32, name="middle_plain", tag="y3", align_bytes=64)
+        for t in (1, 2):
+            plain_copy(t, middle_plain[:, t - 1, :])
+            pulls(t)
+            upper_clamp(t - 1, slice(0, S))
 
         z2_codes = sb.tile([P, S], U32, name="z2_codes", align_bytes=64)
         z2_plane = sb.tile([P, S], U8, name="z2_plane", align_bytes=64)
@@ -183,9 +183,10 @@ def tile_picked_tiepullbmedlerp_none_po_kernel(
                 turn_back(acc, round_and_pair("z2_paired%d" % (2 * h + i), z2_sums[2 * h + i]), i)
             cols = slice(h * HALF, (h + 1) * HALF)
             quantise_half("z2_grouped%d" % h, acc, z2_codes[:, cols], z2_plane[:, cols])
-            plain_copy(2 + h, "z2_paired%d" % (2 * h + 1))
-            pulls(2 + h)
-            upper_clamp(1 + h, slice(0, S))
+        last_plain = sb.tile([P, S], F32, name="last_plain", tag="z2_paired3", align_bytes=64)
+        plain_copy(3, last_plain[:])
+        pulls(3)
+        upper_clamp(2, slice(0, S))
         b = []
         b_plain = sb.tile([P, PACK, S], F32, name="b_plain")
         for t in range(PACK):
@@ -218,11 +219,13 @@ def tile_picked_tiepullbmedlerp_none_po_kernel(
             quantise_half("z_grouped%d" % h, acc, z_codes[:], z_plane[:])
             for t in range(PACK):
                 product(a_acc[t][:, cols], w2, t, z_codes[:], z_plane[:])
+        early_mix = sb.tile([P, 2, S], F32, name="early_mix", tag="z_paired3", align_bytes=64)
         for t in range(PACK):
-            tag = ("mix0", "mix1", "z_grouped0", "z_grouped1")[t]
-            mix.append(sb.tile([P, S], F32, name="mix%d" % t, tag=tag, align_bytes=64))
-            nc.vector.tensor_tensor(mix[t][:], b[t][:].indirect(n7_sb[:]), b_plain[:, t, :], ALU.subtract)
-            nc.scalar.activation(mix[t][:], mix[t][:], ACT.Sigmoid)
+            tag = ("lead0", "lead1", "z_grouped0", "z_grouped1")[t]
+            lead = sb.tile([P, S], F32, name="lead%d" % t, tag=tag, align_bytes=64)
+            nc.vector.tensor_tensor(lead[:], b[t][:].indirect(n7_sb[:]), b_plain[:, t, :], ALU.subtract)
+            mix.append(early_mix[:, t, :] if t < 2 else lead[:])
+            nc.scalar.activation(mix[t], lead[:], ACT.Sigmoid)
 
         a = []
         kept = sb.tile([P, PACK, S], F32, name="kept")
@@ -261,7 +264,7 @@ def tile_picked_tiepullbmedlerp_none_po_kernel(
             a.append(sb.tile([P, S], F32, name="a%d" % t))
             nc.scalar.copy(a[t][:], a_acc[t][:])
             draw(t, 0)
-            nc.vector.scalar_tensor_tensor(kept[:, t, :], mix[t][:], 1.0, a[t][:], ALU.subtract, ALU.mult)
+            nc.vector.scalar_tensor_tensor(kept[:, t, :], mix[t], 1.0, a[t][:], ALU.subtract, ALU.mult)
         g0 = finish(0, 256)
         for t in range(PACK):
             draw(t, 1)

from contextlib import ExitStack

import concourse.mybir as mybir
from concourse.masks import make_identity

K, T, S, H = 512, 2048, 512, 512
FLOPS = 3 * 2 * 512 * 512 * 512

F32 = mybir.dt.float32
BF16 = mybir.dt.bfloat16
I32 = mybir.dt.int32
U32 = mybir.dt.uint32
U16 = mybir.dt.uint16
U8 = mybir.dt.uint8
FP8X4 = mybir.dt.float8_e4m3fn_x4
FP4X4 = mybir.dt.float4_e2m1fn_x4
ALU = mybir.AluOpType
ACT = mybir.ActivationFunctionType

P = 128
PACK = 4
HALF = S // 2
WIDE = 2 * S


def tile_picked_tiepullbmedlerp_none_po_kernel(
    tc, x_words, x_scales, w1_words, w1_scales, gn, w2_words, w2_scales,
    offs, n1, n2, n3, n4, n5, n6, n7, out_0, out_1, out_2,
):
    nc = tc.nc
    with ExitStack() as ctx:
        lists = ctx.enter_context(tc.tile_pool(name="lists", bufs=1))
        sb = ctx.enter_context(tc.tile_pool(name="sb", bufs=1))
        ps = ctx.enter_context(tc.psum_pool(name="ps", bufs=1))

        def load_list(name, src):
            tile = lists.tile([P, S // 16], U16, name=name)
            nc.sync.dma_start(tile[:], src)
            return tile

        def bank(number, name, shape):
            return ps.tile(shape, F32, name=name, tag="bank%d" % number)

        def zeroed_plane(engine, name, width):
            plane = sb.tile([P, width], U8, name=name, tag=name, align_bytes=64)
            engine.memset(plane[:].bitcast(I32), 0)
            return plane

        def load_scale_rows(queues, plane, src):
            for q in range(4):
                queues[q].dma_start(plane[32 * q : 32 * q + 4, :].bitcast(I32), src[0, 4 * q : 4 * q + 4, :].bitcast(I32))

        def deal_words(name, words, tag, pieces):
            dealt = sb.tile([P, PACK, 2 * P], U8, name=name, tag=tag, align_bytes=64)
            step = PACK // pieces
            for t in range(0, PACK, step):
                nc.vector.tensor_copy(
                    dealt[:, t : t + step, :].rearrange("p t (m b) -> p t m b", b=2),
                    words[:].rearrange("p (m t b) -> p t m b", t=PACK, b=2)[:, t : t + step],
                )
            return dealt

        def deal_plane(name, plane, tag):
            dealt = sb.tile([P, PACK, P], U8, name=name, tag=tag, align_bytes=64)
            nc.vector.tensor_copy(dealt[:], plane[:].rearrange("p (m t) -> p t m", t=PACK))
            return dealt

        def product(acc, weights, t, codes, plane):
            nc.tensor.matmul_mx(
                out=acc, lhsT=weights[0][:, t, :].bitcast(FP4X4), lhsT_scale=weights[1][:, t, :],
                rhs=codes.bitcast(FP8X4), rhs_scale=plane, start=True, stop=True,
            )

        x_plane = zeroed_plane(nc.vector, "x_plane", T)
        w1_plane = zeroed_plane(nc.gpsimd, "w1_plane", H)
        offs_sb = load_list("offs_sb", offs)
        w1_sb = sb.tile([P, 2 * H], U8, name="w1_sb")
        nc.sync.dma_start(w1_sb[:].bitcast(I32), w1_words[0].bitcast(I32))
        x_sb = sb.tile([P, T], U32, name="x_sb", tag="x_sb", align_bytes=64)
        nc.sync.dma_start(x_sb[:].bitcast(I32), x_words[0].rearrange("p c r -> p (c r)").bitcast(I32))
        gain = sb.tile([P, PACK], F32, name="gain")
        nc.sync.dma_start(gain[:], gn.rearrange("(p t) o -> p (t o)", t=PACK))
        load_scale_rows([nc.sync] * 4, x_plane, x_scales)
        load_scale_rows([nc.gpsimd, nc.gpsimd, nc.sync, nc.sync], w1_plane, w1_scales)
        w2_plane = zeroed_plane(nc.vector, "w2_plane", H)
        n4_sb = load_list("n4_sb", n4)
        w2_sb = sb.tile([P, 2 * H], U8, name="w2_sb")
        nc.sync.dma_start(w2_sb[:].bitcast(I32), w2_words[0].bitcast(I32))
        n1_sb = load_list("n1_sb", n1)
        n2_sb = load_list("n2_sb", n2)
        n5_sb = load_list("n5_sb", n5)
        n3_sb = load_list("n3_sb", n3)
        load_scale_rows([nc.sync] * 4, w2_plane, w2_scales)
        n7_sb = load_list("n7_sb", n7)
        n6_sb = load_list("n6_sb", n6)
        ident = sb.tile([P, P], F32, name="ident")
        nc.vector.memset(ident[:], 0.0)
        warm = sb.tile([P, 1], F32, name="warm")
        nc.scalar.activation(warm[:], ident[:, 0:1], ACT.Sigmoid)
        make_identity(nc, ident[:], nomemset=True)

        w1_dealt_words = deal_words("w1_dealt_words", w1_sb, "w1_dealt_words", 1)
        picked_plane = sb.tile([P, S], U8, name="picked_plane", align_bytes=64)
        nc.vector.tensor_copy(picked_plane[:], x_plane[:].indirect(offs_sb[:]))
        picked = sb.tile([P, S], U32, name="picked", align_bytes=64)
        nc.vector.tensor_copy(picked[:], x_sb[:].indirect(offs_sb[:]))
        w1 = (w1_dealt_words, deal_plane("w1_dealt_plane", w1_plane, "w1_dealt_plane"))

        def add_turned(acc, term, first, last):
            nc.tensor.matmul(acc, lhsT=term, rhs=ident[:], is_transpose=True, start=first, stop=last)

        def round_and_pair(name, sums):
            paired = sb.tile([P, 2, P, 2], BF16, name=name, tag=name, align_bytes=64)
            nc.scalar.copy(paired[:], sums[:].rearrange("c (u e) p -> c u p e", e=2))
            return paired

        def turn_back(acc, paired, chunk):
            words = paired[:].rearrange("c u p e -> c (u p e)").bitcast(F32)
            for u in range(2):
                nc.tensor.transpose(acc[:, u, chunk * P : (chunk + 1) * P], words[:, u * P : (u + 1) * P], ident[:])

        def quantise_half(name, acc, codes, plane):
            grouped = sb.tile([P, HALF * PACK], BF16, name=name, tag=name, align_bytes=64)
            nc.scalar.copy(grouped[:].bitcast(F32).rearrange("p (c u) -> p c u", u=2), acc[:].rearrange("p u c -> p c u"))
            nc.vector.quantize_mx(out=codes.bitcast(FP8X4), scales=plane, in_=grouped[:])

        gate = sb.tile([P, PACK, S], F32, name="gate")
        rest = sb.tile([P, PACK, S], F32, name="rest")
        far = sb.tile([P, PACK, S], F32, name="far")
        near = sb.tile([P, PACK, S], F32, name="near")
        d1 = sb.tile([P, PACK, S], F32, name="d1")
        d2 = sb.tile([P, PACK, S], F32, name="d2")
        upper = sb.tile([P, PACK, S], F32, name="upper")
        z2_sums = [bank(4 + c, "z2_sums%d" % c, [P, PACK, P]) for c in range(4)]
        gy = []
        gy_plain = []

        def pulls(t):
            nc.vector.tensor_tensor(d1[:, t, :], gy[t][:].indirect(n1_sb[:]), gy_plain[t], ALU.subtract)
            nc.vector.tensor_tensor(d2[:, t, :], gy[t][:].indirect(n2_sb[:]), gy_plain[t], ALU.subtract)

        def upper_clamp(t, cols):
            nc.vector.scalar_tensor_tensor(upper[:, t, cols], d1[:, t, cols], 0.0, d2[:, t, cols], ALU.max, ALU.min)

        def plain_copy(t, plain):
            nc.scalar.copy(plain, gy[t][:, :S])
            gy_plain.append(plain)

        for t in range(PACK):
            y_acc = bank(t, "y_acc%d" % t, [P, S])
            product(y_acc[:], w1, t, picked[:], picked_plane[:])
            y = sb.tile([P, WIDE], F32, name="y%d" % t, tag="y%d" % t, align_bytes=64)
            gy.append(sb.tile([P, WIDE], F32, name="gy%d" % t))
            nc.scalar.activation(gy[t][:, :S], y_acc[:], ACT.Copy, scale=gain[:, t : t + 1])
            nc.scalar.copy(y[:, :S], y_acc[:])
            if t == 0:
                first_plain = sb.tile([P, S], F32, name="first_plain")
                nc.vector.tensor_copy(first_plain[:], gy[0][:, :S])
                gy_plain.append(first_plain[:])
            nc.scalar.activation(gate[:, t, :], y[:].indirect(n4_sb[:]), ACT.Sigmoid)
            nc.scalar.activation(rest[:, t, :], gate[:, t, :], ACT.Copy, bias=1.0, scale=-1.0)
            if t == 0:
                pulls(0)
            nc.vector.tensor_tensor(far[:, t, :], gy[t][:].indirect(n5_sb[:]), gate[:, t, :], ALU.mult)
            nc.vector.tensor_tensor(near[:, t, :], gy[t][:].indirect(n3_sb[:]), rest[:, t, :], ALU.mult)
            for c in range(4):
                cols = slice(c * P, (c + 1) * P)
                add_turned(z2_sums[c][:, t, :], far[:, t, cols], True, False)
                add_turned(z2_sums[c][:, t, :], near[:, t, cols], False, True)

        w2 = (deal_words("w2_dealt_words", w2_sb, "x_sb", 2), deal_plane("w2_dealt_plane", w2_plane, "y1"))
        middle_plain = sb.tile([P, 2, S], F32, name="middle_plain", tag="y3", align_bytes=64)
        for t in (1, 2):
            plain_copy(t, middle_plain[:, t - 1, :])
            pulls(t)
            upper_clamp(t - 1, slice(0, S))

        z2_codes = sb.tile([P, S], U32, name="z2_codes", align_bytes=64)
        z2_plane = sb.tile([P, S], U8, name="z2_plane", align_bytes=64)
        for h in range(2):
            acc = bank(h, "z2_back%d" % h, [P, 2, HALF])
            for i in range(2):
                turn_back(acc, round_and_pair("z2_paired%d" % (2 * h + i), z2_sums[2 * h + i]), i)
            cols = slice(h * HALF, (h + 1) * HALF)
            quantise_half("z2_grouped%d" % h, acc, z2_codes[:, cols], z2_plane[:, cols])
        last_plain = sb.tile([P, S], F32, name="last_plain", tag="z2_paired3", align_bytes=64)
        plain_copy(3, last_plain[:])
        pulls(3)
        upper_clamp(2, slice(0, S))
        b = []
        b_plain = sb.tile([P, PACK, S], F32, name="b_plain")
        for t in range(PACK):
            b_acc = bank(2 + t, "b_acc%d" % t, [P, S])
            product(b_acc[:], w2, t, z2_codes[:], z2_plane[:])
            b.append(sb.tile([P, WIDE], F32, name="b%d" % t))
            nc.scalar.copy(b[t][:, :S], b_acc[:])
            nc.scalar.copy(b_plain[:, t, :], b_acc[:])

        for h in range(2):
            upper_clamp(PACK - 1, slice(h * HALF, (h + 1) * HALF))
        z_sums = [bank((6 + c) % 8, "z_sums%d" % c, [P, PACK, P]) for c in range(4)]
        for c in range(4):
            for t in range(PACK):
                add_turned(z_sums[c][:, t, :], gy[t][:, c * P : (c + 1) * P], t == 0, False)
        a_acc = [bank(4 + t, "a_acc%d" % t, [P, S]) for t in range(PACK)]
        mix = []
        for h in range(2):
            cols = slice(h * HALF, (h + 1) * HALF)
            pull = sb.tile([P, PACK, HALF], F32, name="pull%d" % h)
            nc.vector.scalar_tensor_tensor(pull[:], d1[:, :, cols], 0.0, upper[:, :, cols], ALU.min, ALU.max)
            acc = bank(2 + h, "z_back%d" % h, [P, 2, HALF])
            for i in range(2):
                c = 2 * h + i
                for t in range(PACK):
                    add_turned(z_sums[c][:, t, :], pull[:, t, i * P : (i + 1) * P], False, t == PACK - 1)
                turn_back(acc, round_and_pair("z_paired%d" % c, z_sums[c]), i)
            z_codes = sb.tile([P, HALF], U32, name="z_codes%d" % h, align_bytes=64)
            z_plane = sb.tile([P, HALF], U8, name="z_plane%d" % h, align_bytes=64)
            quantise_half("z_grouped%d" % h, acc, z_codes[:], z_plane[:])
            for t in range(PACK):
                product(a_acc[t][:, cols], w2, t, z_codes[:], z_plane[:])
        early_mix = sb.tile([P, 2, S], F32, name="early_mix", tag="z_paired3", align_bytes=64)
        for t in range(PACK):
            tag = ("lead0", "lead1", "z_grouped0", "z_grouped1")[t]
            lead = sb.tile([P, S], F32, name="lead%d" % t, tag=tag, align_bytes=64)
            nc.vector.tensor_tensor(lead[:], b[t][:].indirect(n7_sb[:]), b_plain[:, t, :], ALU.subtract)
            mix.append(early_mix[:, t, :] if t < 2 else lead[:])
            nc.scalar.activation(mix[t], lead[:], ACT.Sigmoid)

        a = []
        kept = sb.tile([P, PACK, S], F32, name="kept")
        drawn = [sb.tile([P, PACK, HALF], F32, name="drawn%d" % h) for h in range(2)]

        def draw(t, h):
            nc.vector.tensor_tensor(
                drawn[h][:, t, :], a[t][:].indirect(n6_sb[:, h * 16 : (h + 1) * 16]),
                mix[t][:, h * HALF : (h + 1) * HALF], ALU.mult,
            )

        out_rows = out_0.rearrange("(p t) c -> p t c", t=PACK)
        out_words = out_1[0].rearrange("p c r -> p (c r)").bitcast(I32)
        out_codes = sb.tile([P, S], U32, name="out_codes", align_bytes=64)
        out_plane = sb.tile([P, S], U8, name="out_plane", align_bytes=64)

        def finish(lo, hi):
            h = lo // HALF
            result = sb.tile([P, PACK, hi - lo], F32, name="result%d" % lo)
            nc.vector.tensor_tensor(result[:], drawn[h][:, :, lo - h * HALF : hi - h * HALF], kept[:, :, lo:hi], ALU.subtract)
            nc.sync.dma_start(out_rows[:, :, lo:hi], result[:])
            grouped = sb.tile([P, hi - lo, PACK], BF16, name="out_grouped%d" % lo, align_bytes=64)
            nc.scalar.copy(
                grouped[:].rearrange("p (c i) t -> p c t i", i=4), result[:].rearrange("p t (c i) -> p c t i", i=4)
            )
            return grouped

        def hand_on(lo, hi, grouped):
            nc.vector.quantize_mx(
                out=out_codes[:, lo:hi].bitcast(FP8X4), scales=out_plane[:, lo:hi],
                in_=grouped[:].rearrange("p c t -> p (c t)"),
            )
            nc.sync.dma_start(out_words[:, lo:hi], out_codes[:, lo:hi].bitcast(I32))

        for t in range(PACK):
            a.append(sb.tile([P, S], F32, name="a%d" % t))
            nc.scalar.copy(a[t][:], a_acc[t][:])
            draw(t, 0)
            nc.vector.scalar_tensor_tensor(kept[:, t, :], mix[t], 1.0, a[t][:], ALU.subtract, ALU.mult)
        g0 = finish(0, 256)
        for t in range(PACK):
            draw(t, 1)
        g1 = finish(256, 384)
        hand_on(0, 256, g0)
        g2 = finish(384, 512)
        hand_on(256, 384, g1)
        hand_on(384, 512, g2)
        for q in range(4):
            queue = nc.scalar if q % 2 == 0 else nc.sync
            queue.dma_start(out_2[0, 4 * q : 4 * q + 4, :].bitcast(I32), out_plane[32 * q : 32 * q + 4, :].bitcast(I32))
